import numpy as np
import ml_dtypes


def mxq(x, axis, fmt="e4m3"):
    dtype, down = {"e4m3": (ml_dtypes.float8_e4m3fn, 7), "e5m2": (ml_dtypes.float8_e5m2, 14)}[fmt]
    v = np.moveaxis(np.asarray(x, np.float32).astype(ml_dtypes.bfloat16).astype(np.float64), axis, -1)
    blocks = v.reshape(v.shape[:-1] + (-1, 32))
    amax = np.abs(blocks).max(-1, keepdims=True)
    byte = np.maximum(np.where(amax > 0, np.frexp(amax)[1] - 1 + 127, 0) - down, 1)
    scale = np.exp2(byte - 127.0)
    codes = (blocks / scale).astype(np.float32).astype(dtype).astype(np.float64)
    return np.moveaxis((codes * scale).reshape(v.shape), -1, axis)


WIDE = False


def mx_kscale(k):
    if not WIDE:
        return np.ones(k)
    levels = np.array([10, -10, 5, -5, 0])
    if k % 512:
        return np.exp2(np.random.permutation(np.resize(levels, k // 32))).repeat(32)
    a = np.empty((k // 512, 16))
    for p in range(k // 512):
        a[p, :8] = np.random.permutation(np.resize(levels, 8))
        for g in range(8):
            far = levels[np.abs(levels - a[p, g]) >= 10]
            a[p, g + 8] = far[np.random.randint(len(far))]
    return np.exp2(a.ravel()).repeat(32)


def f64(x):
    return np.asarray(x).astype(np.float64)


E2M1 = np.array([0.0, 0.5, 1.0, 1.5, 2.0, 3.0, 4.0, 6.0, -0.0, -0.5, -1.0, -1.5, -2.0, -3.0, -4.0, -6.0])


def pack_weight(w, fmt):
    k, n = w.shape
    w = f64(np.asarray(w, np.float32).astype(ml_dtypes.bfloat16)).reshape(k // 32, 32, n)
    amax = np.abs(w).max(1)
    if fmt == "e4m3":
        byte = np.frexp(amax)[1] - 1 + 127 - 7
    else:
        mant, ex = np.frexp(amax / 6.0)
        byte = np.where(mant > 0.5, ex, ex - 1) + 127
    byte = np.clip(np.where(amax > 0, byte, 1), 1, 254)
    scaled = (w * np.exp2(127.0 - byte)[:, None, :]).reshape(k, n).astype(np.float32)
    by_word = np.ascontiguousarray(scaled.reshape(k // 512, 128, 4, n).transpose(0, 1, 3, 2))
    if fmt == "e4m3":
        words = by_word.astype(ml_dtypes.float8_e4m3fn).view(np.uint8)
    else:
        c = by_word.astype(ml_dtypes.float4_e2m1fn).view(np.uint8) & 0xF
        words = (c[..., 0::2] | (c[..., 1::2] << 4)).reshape(k // 512, 128, 2 * n)
    return np.ascontiguousarray(words), np.ascontiguousarray(byte.astype(np.uint8).reshape(k // 512, 16, n))


def unpack_weight(words, scales, fmt):
    g, _, n = scales.shape
    words = np.ascontiguousarray(words).reshape(g, 128, n, -1)
    if fmt == "e4m3":
        vals = words.view(ml_dtypes.float8_e4m3fn).astype(np.float64)
    else:
        nib = np.empty((g, 128, n, 4), np.uint8)
        nib[..., 0::2] = words & 0xF
        nib[..., 1::2] = words >> 4
        vals = E2M1[nib]
    vals = vals * np.repeat(np.exp2(scales.astype(np.float64) - 127.0), 8, axis=1)[..., None]
    return vals.transpose(0, 1, 3, 2).reshape(g * 512, n)


K, M, T = 1536, 512, 1024


def setup_inputs():
    n = np.random.standard_normal
    s = mx_kscale(K)[:, None]
    x = n((K, T)) * s
    x4 = pack_weight(x, "e2m1")
    rest = x - unpack_weight(*x4, "e2m1")
    p_w4 = pack_weight(n((K, M)) / np.sqrt(K) / s, "e2m1")
    return {
        "x4_words": x4[0],
        "x4_scales": x4[1],
        "xr": (rest).astype(np.float32),
        "w4_words": p_w4[0],
        "w4_scales": p_w4[1],
    }


def reference(x4_words, x4_scales, xr, w4_words, w4_scales):
    x4_ = unpack_weight(x4_words, x4_scales, "e2m1")
    xr_ = mxq(f64(xr), 0, "e4m3")
    w4_ = unpack_weight(w4_words, w4_scales, "e2m1")
    y = x4_.T @ w4_ + xr_.T @ w4_
    return np.maximum(y, 0.0) ** 2

@@ -1,0 +1,168 @@
+from contextlib import ExitStack
+
+import concourse.mybir as mybir
+
+K, T, N = 1536, 1024, 512
+FLOPS = 2 * 2 * K * T * N
+
+F32 = mybir.dt.float32
+BF16 = mybir.dt.bfloat16
+I32 = mybir.dt.int32
+U32 = mybir.dt.uint32
+U8 = mybir.dt.uint8
+FP8X4 = mybir.dt.float8_e4m3fn_x4
+FP4X4 = mybir.dt.float4_e2m1fn_x4
+ACT = mybir.ActivationFunctionType
+
+P = 128
+PASSES = K // 512
+TILES = T // P
+
+
+def tile_mix_xres_tm_relu2_kernel(tc, x4_words, x4_scales, xr, w4_words, w4_scales, out):
+    nc = tc.nc
+    with ExitStack() as ctx:
+        keep = ctx.enter_context(tc.tile_pool(name="keep", bufs=1))
+        psum = ctx.enter_context(tc.psum_pool(name="psum", bufs=1))
+        ctx.enter_context(tc.manual_schedule())
+
+        w4 = keep.tile([P, PASSES, 2 * N], U8, name="w4", align_bytes=64)
+        w4s = keep.tile([P, PASSES, N], U8, name="w4s", align_bytes=64)
+        x4 = keep.tile([P, PASSES, 2 * T], U8, name="x4", align_bytes=64)
+        x4s = keep.tile([P, PASSES, T], U8, name="x4s", align_bytes=64)
+        raw = [keep.tile([P, 4, T], F32, name=f"raw{a}", align_bytes=64) for a in range(PASSES)]
+        bf = [keep.tile([P, T, 4], BF16, name=f"bf{a}", align_bytes=64) for a in range(PASSES)]
+        codes = [keep.tile([P, T], U32, name=f"codes{a}", align_bytes=64) for a in range(PASSES)]
+        scales = [keep.tile([P, T], U8, name=f"scales{a}", align_bytes=64) for a in range(PASSES)]
+        relu = [keep.tile([P, N], F32, name=f"relu{i}", align_bytes=64) for i in range(TILES)]
+        res = [keep.tile([P, N], F32, name=f"res{i}", align_bytes=64) for i in range(TILES)]
+        warm = keep.tile([P, 1], F32, name="warm")
+        acc = [psum.tile([P, N], F32, name=f"acc{i}") for i in range(TILES)]
+
+        nc.vector.memset(w4s[:].rearrange("p a n -> p (a n)").bitcast(I32), 0)
+        nc.vector.memset(x4s[:].rearrange("p a n -> p (a n)").bitcast(I32), 0)
+        nc.vector.memset(warm[:], 0.0)
+
+        def load_words(tile, words):
+            nc.sync.dma_start(
+                out=tile[:].bitcast(I32),
+                in_=words.rearrange("a p n -> p a n").bitcast(I32),
+            )
+
+        def load_scales(queue, tile, rows):
+            for q in range(4):
+                queue.dma_start(
+                    out=tile[:].bitcast(I32)[32 * q : 32 * q + 4, :, :],
+                    in_=rows[:, 4 * q : 4 * q + 4, :].rearrange("a r n -> r a n").bitcast(I32),
+                )
+
+        def load_xr(a, t0, t1):
+            rows = xr[512 * a : 512 * (a + 1), t0:t1]
+            nc.sync.dma_start(out=raw[a][:, :, t0:t1], in_=rows.rearrange("(p j) t -> p j t", j=4))
+
+        def copy(engine_copy, a, t0, t1):
+            engine_copy(out=bf[a][:, t0:t1, :], in_=raw[a][:, :, t0:t1].rearrange("p j t -> p t j"))
+
+        def v_copy(a, t0, t1):
+            copy(nc.vector.tensor_copy, a, t0, t1)
+
+        def s_copy(a, t0, t1):
+            copy(nc.scalar.copy, a, t0, t1)
+
+        def quant(a, t0, t1):
+            nc.vector.quantize_mx(
+                out=codes[a][:, t0:t1].bitcast(FP8X4),
+                scales=scales[a][:, t0:t1],
+                in_=bf[a][:, t0:t1, :].rearrange("p t j -> p (t j)"),
+            )
+
+        def mm_x4(i):
+            for a in range(PASSES):
+                nc.tensor.matmul_mx(
+                    out=acc[i][:],
+                    lhsT=x4[:, a, 2 * P * i : 2 * P * (i + 1)].bitcast(FP4X4),
+                    lhsT_scale=x4s[:, a, P * i : P * (i + 1)],
+                    rhs=w4[:, a, :].bitcast(FP4X4),
+                    rhs_scale=w4s[:, a, :],
+                    start=(a == 0),
+                    stop=False,
+                )
+
+        def mm_xr(a, i):
+            nc.tensor.matmul_mx(
+                out=acc[i][:],
+                lhsT=codes[a][:, P * i : P * (i + 1)].bitcast(FP8X4),
+                lhsT_scale=scales[a][:, P * i : P * (i + 1)],
+                rhs=w4[:, a, :].bitcast(FP4X4),
+                rhs_scale=w4s[:, a, :],
+                start=False,
+                stop=(a == PASSES - 1),
+            )
+
+        def s_relu(i):
+            nc.scalar.activation(out=relu[i][:], in_=acc[i][:], func=ACT.Relu)
+
+        def square_store(i):
+            nc.vector.tensor_mul(out=res[i][:], in0=relu[i][:], in1=relu[i][:])
+            nc.sync.dma_start(out=out[P * i : P * (i + 1), :], in_=res[i][:])
+
+        load_words(w4, w4_words)
+        load_scales(nc.gpsimd, w4s, w4_scales)
+        load_words(x4, x4_words)
+        load_scales(nc.sync, x4s, x4_scales)
+        load_xr(0, 0, 1024)
+        load_xr(1, 0, 512)
+        load_xr(2, 0, 512)
+        load_xr(1, 512, 1024)
+        load_xr(2, 512, 768)
+        load_xr(2, 768, 1024)
+        nc.scalar.activation(out=warm[:], in_=warm[:], func=ACT.Relu)
+
+        for i in range(TILES):
+            mm_x4(i)
+
+        v_copy(0, 0, 256)
+        s_copy(0, 256, 512)
+        v_copy(0, 512, 768)
+        s_copy(0, 768, 1024)
+        for q in range(4):
+            quant(0, 256 * q, 256 * (q + 1))
+            mm_xr(0, 2 * q)
+            mm_xr(0, 2 * q + 1)
+
+        for a in (1, 2):
+            v_copy(a, 0, 256)
+            s_copy(a, 256, 512)
+            for q in range(2):
+                quant(a, 256 * q, 256 * (q + 1))
+                mm_xr(a, 2 * q)
+                mm_xr(a, 2 * q + 1)
+        for i in range(4):
+            s_relu(i)
+        square_store(0)
+        v_copy(1, 512, 768)
+        s_copy(1, 768, 1024)
+        square_store(1)
+        square_store(2)
+        quant(1, 512, 768)
+        mm_xr(1, 4)
+        mm_xr(1, 5)
+        square_store(3)
+        quant(1, 768, 1024)
+        mm_xr(1, 6)
+        mm_xr(1, 7)
+        v_copy(2, 512, 640)
+        s_copy(2, 640, 768)
+        quant(2, 512, 640)
+        mm_xr(2, 4)
+        v_copy(2, 768, 896)
+        s_copy(2, 896, 1024)
+        quant(2, 640, 768)
+        mm_xr(2, 5)
+        quant(2, 768, 896)
+        mm_xr(2, 6)
+        quant(2, 896, 1024)
+        mm_xr(2, 7)
+        for i in range(4, 8):
+            s_relu(i)
+            square_store(i)

@@ -43,8 +43,8 @@ def tile_mix_xres_tm_relu2_kernel(tc, x4_words, x4_scales, xr, w4_words, w4_scal
         nc.vector.memset(x4s[:].rearrange("p a n -> p (a n)").bitcast(I32), 0)
         nc.vector.memset(warm[:], 0.0)
 
-        def load_words(tile, words):
-            nc.sync.dma_start(
+        def load_words(queue, tile, words):
+            queue.dma_start(
                 out=tile[:].bitcast(I32),
                 in_=words.rearrange("a p n -> p a n").bitcast(I32),
             )
@@ -106,59 +106,63 @@ def tile_mix_xres_tm_relu2_kernel(tc, x4_words, x4_scales, xr, w4_words, w4_scal
             nc.vector.tensor_mul(out=res[i][:], in0=relu[i][:], in1=relu[i][:])
             nc.sync.dma_start(out=out[P * i : P * (i + 1), :], in_=res[i][:])
 
-        load_words(w4, w4_words)
-        load_scales(nc.gpsimd, w4s, w4_scales)
-        load_words(x4, x4_words)
+        load_words(nc.sync, w4, w4_words)
+        load_words(nc.gpsimd, x4, x4_words)
+        load_scales(nc.sync, w4s, w4_scales)
         load_scales(nc.sync, x4s, x4_scales)
-        load_xr(0, 0, 1024)
-        load_xr(1, 0, 512)
-        load_xr(2, 0, 512)
+        for a in range(3):
+            load_xr(a, 0, 512)
+        load_xr(0, 512, 1024)
         load_xr(1, 512, 1024)
         load_xr(2, 512, 768)
         load_xr(2, 768, 1024)
         nc.scalar.activation(out=warm[:], in_=warm[:], func=ACT.Relu)
 
-        for i in range(TILES):
+        for i in range(4):
             mm_x4(i)
-
-        v_copy(0, 0, 256)
-        s_copy(0, 256, 512)
-        v_copy(0, 512, 768)
-        s_copy(0, 768, 1024)
-        for q in range(4):
-            quant(0, 256 * q, 256 * (q + 1))
-            mm_xr(0, 2 * q)
-            mm_xr(0, 2 * q + 1)
-
-        for a in (1, 2):
+        for a in range(3):
             v_copy(a, 0, 256)
             s_copy(a, 256, 512)
             for q in range(2):
                 quant(a, 256 * q, 256 * (q + 1))
                 mm_xr(a, 2 * q)
                 mm_xr(a, 2 * q + 1)
-        for i in range(4):
-            s_relu(i)
+            if a == 1:
+                mm_x4(4)
+        for i in range(5, 8):
+            mm_x4(i)
+        s_relu(0)
+        v_copy(0, 512, 768)
         square_store(0)
+        s_copy(0, 768, 1024)
+        quant(0, 512, 768)
+        mm_xr(0, 4)
+        mm_xr(0, 5)
+        s_relu(1)
+        square_store(1)
+        quant(0, 768, 1024)
+        mm_xr(0, 6)
+        mm_xr(0, 7)
+        s_relu(2)
         v_copy(1, 512, 768)
         s_copy(1, 768, 1024)
-        square_store(1)
         square_store(2)
+        s_relu(3)
         quant(1, 512, 768)
         mm_xr(1, 4)
         mm_xr(1, 5)
-        square_store(3)
         quant(1, 768, 1024)
         mm_xr(1, 6)
         mm_xr(1, 7)
         v_copy(2, 512, 640)
         s_copy(2, 640, 768)
+        square_store(3)
         quant(2, 512, 640)
         mm_xr(2, 4)
-        v_copy(2, 768, 896)
-        s_copy(2, 896, 1024)
         quant(2, 640, 768)
         mm_xr(2, 5)
+        v_copy(2, 768, 896)
+        s_copy(2, 896, 1024)
         quant(2, 768, 896)
         mm_xr(2, 6)
         quant(2, 896, 1024)

@@ -30,51 +30,62 @@ def tile_mix_xres_tm_relu2_kernel(tc, x4_words, x4_scales, xr, w4_words, w4_scal
         w4s = keep.tile([P, PASSES, N], U8, name="w4s", align_bytes=64)
         x4 = keep.tile([P, PASSES, 2 * T], U8, name="x4", align_bytes=64)
         x4s = keep.tile([P, PASSES, T], U8, name="x4s", align_bytes=64)
-        raw = [keep.tile([P, 4, T], F32, name=f"raw{a}", align_bytes=64) for a in range(PASSES)]
         bf = [keep.tile([P, T, 4], BF16, name=f"bf{a}", align_bytes=64) for a in range(PASSES)]
         codes = [keep.tile([P, T], U32, name=f"codes{a}", align_bytes=64) for a in range(PASSES)]
         scales = [keep.tile([P, T], U8, name=f"scales{a}", align_bytes=64) for a in range(PASSES)]
-        relu = [keep.tile([P, N], F32, name=f"relu{i}", align_bytes=64) for i in range(TILES)]
+        rel = [keep.tile([P, N], F32, name=f"rel{i}", align_bytes=64) for i in range(TILES)]
         res = [keep.tile([P, N], F32, name=f"res{i}", align_bytes=64) for i in range(TILES)]
         warm = keep.tile([P, 1], F32, name="warm")
         acc = [psum.tile([P, N], F32, name=f"acc{i}") for i in range(TILES)]
 
         nc.vector.memset(w4s[:].rearrange("p a n -> p (a n)").bitcast(I32), 0)
         nc.vector.memset(x4s[:].rearrange("p a n -> p (a n)").bitcast(I32), 0)
-        nc.vector.memset(warm[:], 0.0)
+        nc.gpsimd.memset(warm[:], 0.0)
 
-        def load_words(queue, tile, words):
-            queue.dma_start(
-                out=tile[:].bitcast(I32),
-                in_=words.rearrange("a p n -> p a n").bitcast(I32),
+        def load_w4(a0, a1):
+            nc.sync.dma_start(
+                out=w4[:, a0:a1, :].bitcast(I32),
+                in_=w4_words[a0:a1].rearrange("a p n -> p a n").bitcast(I32),
             )
 
-        def load_scales(queue, tile, rows):
+        def load_scales(tile, rows):
             for q in range(4):
-                queue.dma_start(
+                nc.sync.dma_start(
                     out=tile[:].bitcast(I32)[32 * q : 32 * q + 4, :, :],
                     in_=rows[:, 4 * q : 4 * q + 4, :].rearrange("a r n -> r a n").bitcast(I32),
                 )
 
-        def load_xr(a, t0, t1):
-            rows = xr[512 * a : 512 * (a + 1), t0:t1]
-            nc.sync.dma_start(out=raw[a][:, :, t0:t1], in_=rows.rearrange("(p j) t -> p j t", j=4))
+        raw = {}
 
-        def copy(engine_copy, a, t0, t1):
-            engine_copy(out=bf[a][:, t0:t1, :], in_=raw[a][:, :, t0:t1].rearrange("p j t -> p t j"))
+        def load_xr(a, i0, i1):
+            tile = keep.tile([P, 4, P * (i1 - i0)], F32, name=f"raw{a}_{i0}", align_bytes=64)
+            rows = xr[512 * a : 512 * (a + 1), P * i0 : P * i1]
+            nc.sync.dma_start(out=tile[:], in_=rows.rearrange("(p j) t -> p j t", j=4))
+            for i in range(i0, i1):
+                raw[a, i] = (tile, P * (i - i0))
 
-        def v_copy(a, t0, t1):
-            copy(nc.vector.tensor_copy, a, t0, t1)
-
-        def s_copy(a, t0, t1):
-            copy(nc.scalar.copy, a, t0, t1)
-
-        def quant(a, t0, t1):
-            nc.vector.quantize_mx(
-                out=codes[a][:, t0:t1].bitcast(FP8X4),
-                scales=scales[a][:, t0:t1],
-                in_=bf[a][:, t0:t1, :].rearrange("p t j -> p (t j)"),
+        def copy(engine_copy, a, i0, i1):
+            tile, t0 = raw[a, i0]
+            engine_copy(
+                out=bf[a][:, P * i0 : P * i1, :].rearrange("p (c i) j -> p c j i", i=4),
+                in_=tile[:, :, t0 : t0 + P * (i1 - i0)].rearrange("p j (c i) -> p c j i", i=4),
             )
+
+        def v_copy(a, i0, i1):
+            copy(nc.vector.tensor_copy, a, i0, i1)
+
+        def s_copy(a, i0, i1):
+            copy(nc.scalar.copy, a, i0, i1)
+
+        def quant(a, i0, i1):
+            cols = slice(P * i0, P * i1)
+            nc.vector.quantize_mx(
+                out=codes[a][:, cols].bitcast(FP8X4),
+                scales=scales[a][:, cols],
+                in_=bf[a][:, cols, :].rearrange("p t j -> p (t j)"),
+            )
+            for i in range(i0, i1):
+                mm_xr(a, i)
 
         def mm_x4(i):
             for a in range(PASSES):
@@ -99,74 +110,85 @@ def tile_mix_xres_tm_relu2_kernel(tc, x4_words, x4_scales, xr, w4_words, w4_scal
                 stop=(a == PASSES - 1),
             )
 
-        def s_relu(i):
-            nc.scalar.activation(out=relu[i][:], in_=acc[i][:], func=ACT.Relu)
+        def relu(i, cols=slice(0, N)):
+            nc.scalar.activation(out=rel[i][:, cols], in_=acc[i][:, cols], func=ACT.Relu)
 
-        def square_store(i):
-            nc.vector.tensor_mul(out=res[i][:], in0=relu[i][:], in1=relu[i][:])
-            nc.sync.dma_start(out=out[P * i : P * (i + 1), :], in_=res[i][:])
+        def v_square(i, cols=slice(0, N)):
+            nc.vector.tensor_mul(out=res[i][:, cols], in0=rel[i][:, cols], in1=rel[i][:, cols])
 
-        load_words(nc.sync, w4, w4_words)
-        load_words(nc.gpsimd, x4, x4_words)
-        load_scales(nc.sync, w4s, w4_scales)
-        load_scales(nc.sync, x4s, x4_scales)
-        for a in range(3):
-            load_xr(a, 0, 512)
-        load_xr(0, 512, 1024)
-        load_xr(1, 512, 1024)
-        load_xr(2, 512, 768)
-        load_xr(2, 768, 1024)
+        def s_square(i, cols=slice(0, N)):
+            nc.scalar.activation(out=res[i][:, cols], in_=rel[i][:, cols], func=ACT.Square)
+
+        def store(i, cols=slice(0, N)):
+            nc.sync.dma_start(out=out[P * i : P * (i + 1), cols], in_=res[i][:, cols])
+
+        load_w4(0, 1)
+        load_scales(w4s, w4_scales)
+        nc.sync.dma_start(out=x4[:].bitcast(I32), in_=x4_words.rearrange("a p n -> p a n").bitcast(I32))
+        load_w4(1, 3)
+        load_scales(x4s, x4_scales)
+        for a in range(PASSES):
+            load_xr(a, 0, 4)
+        load_xr(0, 4, 8)
+        load_xr(1, 4, 8)
+        load_xr(2, 4, 6)
+        load_xr(2, 6, 7)
+        load_xr(2, 7, 8)
         nc.scalar.activation(out=warm[:], in_=warm[:], func=ACT.Relu)
 
         for i in range(4):
             mm_x4(i)
-        for a in range(3):
-            v_copy(a, 0, 256)
-            s_copy(a, 256, 512)
-            for q in range(2):
-                quant(a, 256 * q, 256 * (q + 1))
-                mm_xr(a, 2 * q)
-                mm_xr(a, 2 * q + 1)
+        for a in range(PASSES):
+            v_copy(a, 0, 2)
+            s_copy(a, 3, 4)
+            v_copy(a, 2, 3)
+            quant(a, 0, 2)
+            quant(a, 2, 4)
             if a == 1:
                 mm_x4(4)
         for i in range(5, 8):
             mm_x4(i)
-        s_relu(0)
-        v_copy(0, 512, 768)
-        square_store(0)
-        s_copy(0, 768, 1024)
-        quant(0, 512, 768)
-        mm_xr(0, 4)
-        mm_xr(0, 5)
-        s_relu(1)
-        square_store(1)
-        quant(0, 768, 1024)
-        mm_xr(0, 6)
-        mm_xr(0, 7)
-        s_relu(2)
-        v_copy(1, 512, 768)
-        s_copy(1, 768, 1024)
-        square_store(2)
-        s_relu(3)
-        quant(1, 512, 768)
-        mm_xr(1, 4)
-        mm_xr(1, 5)
-        quant(1, 768, 1024)
-        mm_xr(1, 6)
-        mm_xr(1, 7)
-        v_copy(2, 512, 640)
-        s_copy(2, 640, 768)
-        square_store(3)
-        quant(2, 512, 640)
-        mm_xr(2, 4)
-        quant(2, 640, 768)
-        mm_xr(2, 5)
-        v_copy(2, 768, 896)
-        s_copy(2, 896, 1024)
-        quant(2, 768, 896)
-        mm_xr(2, 6)
-        quant(2, 896, 1024)
-        mm_xr(2, 7)
-        for i in range(4, 8):
-            s_relu(i)
-            square_store(i)
+
+        relu(0)
+        relu(1)
+        s_square(0)
+        relu(2)
+        s_square(1)
+        v_copy(0, 4, 6)
+        v_copy(0, 6, 8)
+        quant(0, 4, 6)
+        quant(0, 6, 8)
+        s_copy(1, 7, 8)
+        relu(3)
+        s_square(2)
+        s_square(3)
+        for i in range(4):
+            store(i)
+        v_copy(1, 4, 6)
+        v_copy(1, 6, 7)
+        quant(1, 4, 6)
+        quant(1, 6, 8)
+        v_copy(2, 4, 5)
+        v_copy(2, 5, 6)
+        quant(2, 4, 5)
+        quant(2, 5, 6)
+        v_copy(2, 6, 7)
+        relu(4)
+        quant(2, 6, 7)
+        v_copy(2, 7, 8)
+        v_square(4)
+        store(4)
+        quant(2, 7, 8)
+        relu(5)
+        v_square(5)
+        store(5)
+        relu(6)
+        v_square(6)
+        store(6)
+        halves = [slice(0, N // 2), slice(N // 2, N)]
+        relu(7, halves[0])
+        relu(7, halves[1])
+        v_square(7, halves[0])
+        s_square(7, halves[1])
+        store(7, halves[0])
+        store(7, halves[1])

@@ -42,11 +42,8 @@ def tile_mix_xres_tm_relu2_kernel(tc, x4_words, x4_scales, xr, w4_words, w4_scal
         nc.vector.memset(x4s[:].rearrange("p a n -> p (a n)").bitcast(I32), 0)
         nc.gpsimd.memset(warm[:], 0.0)
 
-        def load_w4(a0, a1):
-            nc.sync.dma_start(
-                out=w4[:, a0:a1, :].bitcast(I32),
-                in_=w4_words[a0:a1].rearrange("a p n -> p a n").bitcast(I32),
-            )
+        def load_words(tile, words):
+            nc.sync.dma_start(out=tile[:].bitcast(I32), in_=words.rearrange("a p n -> p a n").bitcast(I32))
 
         def load_scales(tile, rows):
             for q in range(4):
@@ -95,7 +92,7 @@ def tile_mix_xres_tm_relu2_kernel(tc, x4_words, x4_scales, xr, w4_words, w4_scal
                     lhsT_scale=x4s[:, a, P * i : P * (i + 1)],
                     rhs=w4[:, a, :].bitcast(FP4X4),
                     rhs_scale=w4s[:, a, :],
-                    start=(a == 0),
+                    start=(a == 0 and i >= 4),
                     stop=False,
                 )
 
@@ -106,7 +103,7 @@ def tile_mix_xres_tm_relu2_kernel(tc, x4_words, x4_scales, xr, w4_words, w4_scal
                 lhsT_scale=scales[a][:, P * i : P * (i + 1)],
                 rhs=w4[:, a, :].bitcast(FP4X4),
                 rhs_scale=w4s[:, a, :],
-                start=False,
+                start=(a == 0 and i < 4),
                 stop=(a == PASSES - 1),
             )
 
@@ -122,73 +119,76 @@ def tile_mix_xres_tm_relu2_kernel(tc, x4_words, x4_scales, xr, w4_words, w4_scal
         def store(i, cols=slice(0, N)):
             nc.sync.dma_start(out=out[P * i : P * (i + 1), cols], in_=res[i][:, cols])
 
-        load_w4(0, 1)
+        nc.scalar.activation(out=warm[:], in_=warm[:], func=ACT.Relu)
+        load_words(w4, w4_words)
         load_scales(w4s, w4_scales)
-        nc.sync.dma_start(out=x4[:].bitcast(I32), in_=x4_words.rearrange("a p n -> p a n").bitcast(I32))
-        load_w4(1, 3)
+        load_xr(0, 0, 4)
+        load_words(x4, x4_words)
         load_scales(x4s, x4_scales)
-        for a in range(PASSES):
-            load_xr(a, 0, 4)
+        load_xr(1, 0, 4)
+        load_xr(2, 0, 4)
         load_xr(0, 4, 8)
         load_xr(1, 4, 8)
         load_xr(2, 4, 6)
-        load_xr(2, 6, 7)
-        load_xr(2, 7, 8)
-        nc.scalar.activation(out=warm[:], in_=warm[:], func=ACT.Relu)
+        load_xr(2, 6, 8)
 
-        for i in range(4):
-            mm_x4(i)
+        for i in range(6):
+            nc.tensor.matmul_mx(
+                out=acc[7][:],
+                lhsT=w4[:, 0, : 2 * P].bitcast(FP4X4),
+                lhsT_scale=w4s[:, 0, :P],
+                rhs=w4[:, 0, :].bitcast(FP4X4),
+                rhs_scale=w4s[:, 0, :],
+                start=True,
+                stop=True,
+            )
         for a in range(PASSES):
             v_copy(a, 0, 2)
-            s_copy(a, 3, 4)
-            v_copy(a, 2, 3)
+            s_copy(a, 2, 4)
             quant(a, 0, 2)
             quant(a, 2, 4)
-            if a == 1:
-                mm_x4(4)
-        for i in range(5, 8):
+            if a == 0:
+                for i in range(4):
+                    mm_x4(i)
+        for i in range(4, 8):
             mm_x4(i)
 
         relu(0)
-        relu(1)
-        s_square(0)
-        relu(2)
-        s_square(1)
+        for i in range(1, 4):
+            relu(i)
+            s_square(i - 1)
+        s_square(3)
+        for i in range(4):
+            store(i)
+
         v_copy(0, 4, 6)
         v_copy(0, 6, 8)
         quant(0, 4, 6)
         quant(0, 6, 8)
-        s_copy(1, 7, 8)
-        relu(3)
-        s_square(2)
-        s_square(3)
-        for i in range(4):
-            store(i)
         v_copy(1, 4, 6)
         v_copy(1, 6, 7)
+        s_copy(1, 7, 8)
+        v_copy(2, 4, 6)
+        s_copy(2, 6, 7)
         quant(1, 4, 6)
-        quant(1, 6, 8)
-        v_copy(2, 4, 5)
-        v_copy(2, 5, 6)
         quant(2, 4, 5)
         quant(2, 5, 6)
-        v_copy(2, 6, 7)
-        relu(4)
-        quant(2, 6, 7)
+        quant(1, 6, 8)
         v_copy(2, 7, 8)
+        quant(2, 6, 7)
+        quant(2, 7, 8)
+        relu(4)
+        relu(5)
+        relu(6)
         v_square(4)
         store(4)
-        quant(2, 7, 8)
-        relu(5)
         v_square(5)
         store(5)
-        relu(6)
-        v_square(6)
+        s_square(6)
         store(6)
-        halves = [slice(0, N // 2), slice(N // 2, N)]
-        relu(7, halves[0])
-        relu(7, halves[1])
-        v_square(7, halves[0])
-        s_square(7, halves[1])
-        store(7, halves[0])
-        store(7, halves[1])
+        nc.vector.tensor_scalar_max(out=rel[7][:], in0=acc[7][:], scalar1=0.0)
+        left, right = slice(0, N // 2), slice(N // 2, N)
+        v_square(7, left)
+        s_square(7, right)
+        store(7, left)
+        store(7, right)

from contextlib import ExitStack

import concourse.mybir as mybir

K, T, N = 1536, 1024, 512
FLOPS = 2 * 2 * K * T * N

F32 = mybir.dt.float32
BF16 = mybir.dt.bfloat16
I32 = mybir.dt.int32
U32 = mybir.dt.uint32
U8 = mybir.dt.uint8
FP8X4 = mybir.dt.float8_e4m3fn_x4
FP4X4 = mybir.dt.float4_e2m1fn_x4
ACT = mybir.ActivationFunctionType

P = 128
PASSES = K // 512
TILES = T // P


def tile_mix_xres_tm_relu2_kernel(tc, x4_words, x4_scales, xr, w4_words, w4_scales, out):
    nc = tc.nc
    with ExitStack() as ctx:
        keep = ctx.enter_context(tc.tile_pool(name="keep", bufs=1))
        psum = ctx.enter_context(tc.psum_pool(name="psum", bufs=1))
        ctx.enter_context(tc.manual_schedule())

        w4 = keep.tile([P, PASSES, 2 * N], U8, name="w4", align_bytes=64)
        w4s = keep.tile([P, PASSES, N], U8, name="w4s", align_bytes=64)
        x4 = keep.tile([P, PASSES, 2 * T], U8, name="x4", align_bytes=64)
        x4s = keep.tile([P, PASSES, T], U8, name="x4s", align_bytes=64)
        bf = [keep.tile([P, T, 4], BF16, name=f"bf{a}", align_bytes=64) for a in range(PASSES)]
        codes = [keep.tile([P, T], U32, name=f"codes{a}", align_bytes=64) for a in range(PASSES)]
        scales = [keep.tile([P, T], U8, name=f"scales{a}", align_bytes=64) for a in range(PASSES)]
        rel = [keep.tile([P, N], F32, name=f"rel{i}", align_bytes=64) for i in range(TILES)]
        res = [keep.tile([P, N], F32, name=f"res{i}", align_bytes=64) for i in range(TILES)]
        warm = keep.tile([P, 1], F32, name="warm")
        acc = [psum.tile([P, N], F32, name=f"acc{i}") for i in range(TILES)]

        nc.vector.memset(w4s[:].rearrange("p a n -> p (a n)").bitcast(I32), 0)
        nc.vector.memset(x4s[:].rearrange("p a n -> p (a n)").bitcast(I32), 0)
        nc.gpsimd.memset(warm[:], 0.0)

        def load_words(tile, words):
            nc.sync.dma_start(out=tile[:].bitcast(I32), in_=words.rearrange("a p n -> p a n").bitcast(I32))

        def load_scales(tile, rows):
            for q in range(4):
                nc.sync.dma_start(
                    out=tile[:].bitcast(I32)[32 * q : 32 * q + 4, :, :],
                    in_=rows[:, 4 * q : 4 * q + 4, :].rearrange("a r n -> r a n").bitcast(I32),
                )

        raw = {}

        def load_xr(a, i0, i1):
            tile = keep.tile([P, 4, P * (i1 - i0)], F32, name=f"raw{a}_{i0}", align_bytes=64)
            rows = xr[512 * a : 512 * (a + 1), P * i0 : P * i1]
            nc.sync.dma_start(out=tile[:], in_=rows.rearrange("(p j) t -> p j t", j=4))
            for i in range(i0, i1):
                raw[a, i] = (tile, P * (i - i0))

        def copy(engine_copy, a, i0, i1):
            tile, t0 = raw[a, i0]
            engine_copy(
                out=bf[a][:, P * i0 : P * i1, :].rearrange("p (c i) j -> p c j i", i=4),
                in_=tile[:, :, t0 : t0 + P * (i1 - i0)].rearrange("p j (c i) -> p c j i", i=4),
            )

        def v_copy(a, i0, i1):
            copy(nc.vector.tensor_copy, a, i0, i1)

        def s_copy(a, i0, i1):
            copy(nc.scalar.copy, a, i0, i1)

        def quant(a, i0, i1):
            cols = slice(P * i0, P * i1)
            nc.vector.quantize_mx(
                out=codes[a][:, cols].bitcast(FP8X4),
                scales=scales[a][:, cols],
                in_=bf[a][:, cols, :].rearrange("p t j -> p (t j)"),
            )
            for i in range(i0, i1):
                mm_xr(a, i)

        def mm_x4(i):
            for a in range(PASSES):
                nc.tensor.matmul_mx(
                    out=acc[i][:],
                    lhsT=x4[:, a, 2 * P * i : 2 * P * (i + 1)].bitcast(FP4X4),
                    lhsT_scale=x4s[:, a, P * i : P * (i + 1)],
                    rhs=w4[:, a, :].bitcast(FP4X4),
                    rhs_scale=w4s[:, a, :],
                    start=(a == 0 and i >= 4),
                    stop=False,
                )

        def mm_xr(a, i):
            nc.tensor.matmul_mx(
                out=acc[i][:],
                lhsT=codes[a][:, P * i : P * (i + 1)].bitcast(FP8X4),
                lhsT_scale=scales[a][:, P * i : P * (i + 1)],
                rhs=w4[:, a, :].bitcast(FP4X4),
                rhs_scale=w4s[:, a, :],
                start=(a == 0 and i < 4),
                stop=(a == PASSES - 1),
            )

        def relu(i, cols=slice(0, N)):
            nc.scalar.activation(out=rel[i][:, cols], in_=acc[i][:, cols], func=ACT.Relu)

        def v_square(i, cols=slice(0, N)):
            nc.vector.tensor_mul(out=res[i][:, cols], in0=rel[i][:, cols], in1=rel[i][:, cols])

        def s_square(i, cols=slice(0, N)):
            nc.scalar.activation(out=res[i][:, cols], in_=rel[i][:, cols], func=ACT.Square)

        def store(i, cols=slice(0, N)):
            nc.sync.dma_start(out=out[P * i : P * (i + 1), cols], in_=res[i][:, cols])

        nc.scalar.activation(out=warm[:], in_=warm[:], func=ACT.Relu)
        load_words(w4, w4_words)
        load_scales(w4s, w4_scales)
        load_xr(0, 0, 4)
        load_words(x4, x4_words)
        load_scales(x4s, x4_scales)
        load_xr(1, 0, 4)
        load_xr(2, 0, 4)
        load_xr(0, 4, 8)
        load_xr(1, 4, 8)
        load_xr(2, 4, 6)
        load_xr(2, 6, 8)

        for i in range(6):
            nc.tensor.matmul_mx(
                out=acc[7][:],
                lhsT=w4[:, 0, : 2 * P].bitcast(FP4X4),
                lhsT_scale=w4s[:, 0, :P],
                rhs=w4[:, 0, :].bitcast(FP4X4),
                rhs_scale=w4s[:, 0, :],
                start=True,
                stop=True,
            )
        for a in range(PASSES):
            v_copy(a, 0, 2)
            s_copy(a, 2, 4)
            quant(a, 0, 2)
            quant(a, 2, 4)
            if a == 0:
                for i in range(4):
                    mm_x4(i)
        for i in range(4, 8):
            mm_x4(i)

        relu(0)
        for i in range(1, 4):
            relu(i)
            s_square(i - 1)
        s_square(3)
        for i in range(4):
            store(i)

        v_copy(0, 4, 6)
        v_copy(0, 6, 8)
        quant(0, 4, 6)
        quant(0, 6, 8)
        v_copy(1, 4, 6)
        v_copy(1, 6, 7)
        s_copy(1, 7, 8)
        v_copy(2, 4, 6)
        s_copy(2, 6, 7)
        quant(1, 4, 6)
        quant(2, 4, 5)
        quant(2, 5, 6)
        quant(1, 6, 8)
        v_copy(2, 7, 8)
        quant(2, 6, 7)
        quant(2, 7, 8)
        relu(4)
        relu(5)
        relu(6)
        v_square(4)
        store(4)
        v_square(5)
        store(5)
        s_square(6)
        store(6)
        nc.vector.tensor_scalar_max(out=rel[7][:], in0=acc[7][:], scalar1=0.0)
        left, right = slice(0, N // 2), slice(N // 2, N)
        v_square(7, left)
        s_square(7, right)
        store(7, left)
        store(7, right)
